import numpy as np, ml_dtypes
CORES = [40,64,80,88,96,104,120,144]
N = 8
NB, B = 3, 512
def setup_inputs(rng):
    return {"x": rng.standard_normal((N, 128, NB * B), dtype=np.float32).astype(ml_dtypes.bfloat16), "wv": (rng.standard_normal((N, 128, 128), dtype=np.float32) / 16).astype(ml_dtypes.bfloat16), "wh": (rng.standard_normal((N, 128, 128), dtype=np.float32) / 16).astype(ml_dtypes.bfloat16)}
def setup_inputs_big(rng):
    d = setup_inputs(rng)
    for k in ("x",): d[k] = (d[k].astype(np.float32) * 1048576.0).astype(d[k].dtype)
    return d
def setup_inputs_small(rng):
    d = setup_inputs(rng)
    for k in ("x",): d[k] = (d[k].astype(np.float32) * (1 / 1048576.0)).astype(d[k].dtype)
    return d
def setup_inputs_apart(rng):
    d = setup_inputs(rng)
    f = (10.0 ** rng.permutation(np.linspace(-1.5, 1.5, N))).astype(np.float32).reshape(N, 1, 1)
    for k in ("x",): d[k] = (d[k].astype(np.float32) * f).astype(d[k].dtype)
    return d
def reference(x, wv, wh):
    X, WV, WH = x.astype(np.float64), wv.astype(np.float64), wh.astype(np.float64)
    h = np.zeros((N, NB, 128, B))
    for r in range(N):
        for c in range(NB):
            a = X[r][:, B * c:B * c + B].copy()
            if r: a += WV[r].T @ h[r - 1][c]
            if c: a += WH[r].T @ h[r][c - 1]
            h[r][c] = np.maximum(a, 0.0)
    return {"y": np.concatenate([h[:, c] for c in range(NB)], axis=2).astype(ml_dtypes.bfloat16)}

@@ -1,0 +1,169 @@
+from concourse.bass import DstId, RemoteDMATransfer
+from concourse.mybir import AluOpType
+
+NB, B, NR = 3, 512, 8
+SL = B // NR
+
+SCRATCH = {
+    "xin":  ("sbuf", [128, NB, NR, SL], "bfloat16"),
+    "xs":   ("sbuf", [128, NR, NB, SL], "bfloat16"),
+    "RX":   ("sbuf", [128, 2, NB, SL], "bfloat16"),
+    "X":    ("sbuf", [128, NR, NB, SL], "bfloat16"),
+    "Wt":   ("sbuf", [128, NR, 256], "bfloat16"),
+    "H":    ("sbuf", [128, NR * NB, SL], "bfloat16"),
+    "land": ("sbuf", [128, NR, NB, SL], "bfloat16"),
+    "yb":   ("sbuf", [128, NB, NR, SL], "bfloat16"),
+    "Zb":   ("sbuf", [128, 129], "bfloat16"),
+    "Id":   ("sbuf", [128, 128], "bfloat16"),
+    "Zr":   ("sbuf", [128, SL], "float32"),
+    "D":    ("dram", [129, 128], "bfloat16"),
+    "P00":  ("psum", [128, 512], "float32"), "P01": ("psum", [128, 512], "float32"), "P02": ("psum", [128, 512], "float32"),
+    "P10":  ("psum", [128, 512], "float32"), "P11": ("psum", [128, 512], "float32"), "P12": ("psum", [128, 512], "float32"),
+}
+SEMAPHORES = (["lw", "lx0", "lx1", "lx2", "sxc", "sxd", "ls", "rw", "rx", "ret", "cp0", "cp1", "cp2", "st",
+               "ms", "d1", "d2", "p0", "p1", "p2", "v0", "v1", "v2"] + ["a%d" % r for r in range(NR)])
+
+
+def _bits(mask):
+    return [1 << i for i in range(mask.bit_length()) if (mask >> i) & 1]
+
+
+def _plan(T, topo):
+    c0 = list(T.cores)
+    world = range((max(topo.host(c) for c in c0) + 1) * topo.CORES_PER_HOST)
+    wa, rb = [], []
+    for r in range(NR):
+        free = [c for c in world if c != c0[r] and topo.host(c) == topo.host(c0[r]) and topo.chip(c) == topo.chip(c0[r])
+                and all(topo.may_write(c, d) for d in c0)]
+        wa.append([c for c in free if topo.die(c) == topo.die(c0[r])][0])
+        rb.append([c for c in free if topo.die(c) != topo.die(c0[r])][0])
+    order = sorted(range(NR), key=lambda s: (not topo.may_write(c0[0], wa[s]), s))
+    sl = [order.index(s) for s in range(NR)]
+    direct = [[s for s in order if s != r and topo.may_write(c0[r], wa[s])] for r in range(NR)]
+    cross = [[s for s in order if not topo.may_write(c0[r], wa[s])] for r in range(NR)]
+    return c0, wa, rb, sl, direct, cross
+
+
+def _tr(topo, src_core, dsts, mask_bits, sem, src):
+    ids = []
+    for d, _ in dsts:
+        rid, pid = topo.addr(d, src_core)
+        ids.append(DstId(rid=rid, pnc=pid))
+    return RemoteDMATransfer(dst_ids=ids, dma_engine_mask=sum(mask_bits), remote_sem=sem, srcs=[src], dsts=[ap for _, ap in dsts])
+
+
+def rank_program(g, core, T, topo):
+    c0, wa, rb, sl, direct, cross = _plan(T, topo)
+    S = T.sem
+    sy, sc, ve, te = g.sync, g.scalar, g.vector, g.tensor
+    wlo = lambda r: 128 if r == 0 else 0
+    W = lambda r: T.Wt[:, r, wlo(r):256]
+
+    if core in c0:
+        r = c0.index(core)
+        A, Bc = wa[r], rb[r]
+        d1, d2, d3 = direct[r]
+        off = _bits(topo.mask(core, wa[d1]))
+        up = [b for b in _bits(topo.mask(core, A)) if b not in off]
+        hu = len(up) // 2
+        clo, dlo = sl[cross[r][0]], min(sl[s] for s in direct[r] + [r])
+        nlw = 16
+        if r > 0:
+            sy.dma_start(T.Wt[:, r, 0:128], T.wv[:]).then_inc(S.lw, 16)
+            nlw = 32
+        sy.dma_start(T.Wt[:, r, 128:256], T.wh[:]).then_inc(S.lw, 16)
+        for c, q in ((0, sc), (1, sy), (2, sc)):
+            q.dma_start(T.xin[:, c], T.x[:, c * B:(c + 1) * B]).then_inc(S["lx%d" % c], 16)
+        for c in range(NB):
+            ve.wait_ge(S["lx%d" % c], 16)
+            ve.tensor_copy(T.xs[:, clo:clo + 4, c, :], T.xin[:, c, clo:clo + 4, :]).then_inc(S.sxc, 1)
+        for c in range(NB):
+            ve.tensor_copy(T.xs[:, dlo:dlo + 4, c, :], T.xin[:, c, dlo:dlo + 4, :]).then_inc(S.sxd, 1)
+        g.wait_ge(S.lw, nlw)
+        g.remote_dma_fused([_tr(topo, core, [(A, W(r))], up[:hu], S.rw, W(r)),
+                            _tr(topo, core, [(Bc, W(r))], up[hu:], S.rw, W(r))], local_sem=S.ls)
+        g.wait_ge(S.sxc, NB)
+        g.remote_dma_fused([_tr(topo, core, [(A, T.RX[:])], up[:hu], S.rx, T.xs[:, clo:clo + 2]),
+                            _tr(topo, core, [(Bc, T.RX[:])], up[hu:], S.rx, T.xs[:, clo + 2:clo + 4])], local_sem=S.ls)
+        g.remote_dma_fused([_tr(topo, core, [(wa[d1], W(r)), (wa[d2], W(r))], off[0:4], S["a%d" % r], W(r)),
+                            _tr(topo, core, [(wa[d3], W(r))], off[4:8], S["a%d" % r], W(r))], local_sem=S.ls)
+        g.wait_ge(S.sxd, NB)
+        g.remote_dma_fused([_tr(topo, core, [(wa[d3], T.X[:, r])], off[0:4], S["a%d" % r], T.xs[:, sl[d3]]),
+                            _tr(topo, core, [(wa[d1], T.X[:, r])], off[4:6], S["a%d" % r], T.xs[:, sl[d1]]),
+                            _tr(topo, core, [(wa[d2], T.X[:, r])], off[6:8], S["a%d" % r], T.xs[:, sl[d2]]),
+                            _tr(topo, core, [(A, T.X[:, r])], up, S["a%d" % r], T.xs[:, sl[r]])], local_sem=S.ls)
+        g.wait_ge(S.ls, 2 * len(up) + 8 + 8 + len(up))
+        ve.wait_ge(S.ret, 4 * NR)
+        for c, q in ((0, sy), (1, sc), (2, sy)):
+            ve.tensor_copy(T.yb[:, c], T.land[:, :, c, :]).then_inc(S["cp%d" % c], 1)
+            q.wait_ge(S["cp%d" % c], 1)
+            q.dma_start(T.y[:, c * B:(c + 1) * B], T.yb[:, c]).then_inc(S.st, 16)
+        g.wait_ge(S.st, 16 * NB)
+        return
+
+    if core not in wa and core not in rb:
+        return
+
+    is_a = core in wa
+    s = wa.index(core) if is_a else rb.index(core)
+    mine = cross[s][0:2] if is_a else cross[s][2:4]
+    hu = len([b for b in _bits(topo.mask(c0[s], core)) if b not in _bits(topo.mask(c0[s], wa[direct[s][0]]))]) // 2
+    off = _bits(topo.mask(core, wa[mine[0]]))
+    g.wait_ge(S.rw, hu)
+    g.remote_dma_fused([_tr(topo, core, [(wa[mine[k]], W(s))], off[4 * k:4 * k + 4], S["a%d" % s], W(s)) for k in range(2)],
+                       local_sem=S.ls)
+    g.wait_ge(S.rx, hu)
+    g.remote_dma_fused([_tr(topo, core, [(wa[mine[k]], T.X[:, s])], off[4 * k:4 * k + 4], S["a%d" % s], T.RX[:, k])
+                        for k in range(2)], local_sem=S.ls)
+    if not is_a:
+        g.wait_ge(S.ls, 16)
+        return
+
+    def arrived(r):
+        if r == s:
+            return 2 * hu
+        if s in cross[r]:
+            return 8
+        return 4 + (4 if s == direct[r][2] else 2)
+
+    ve.memset(T.Zb[:], 0.0).then_inc(S.ms, 1)
+    ve.wait_ge(S.ms, 1)
+    ve.memset(T.Zb[:, 0:1], 1.0).then_inc(S.ms, 1)
+    ve.memset(T.Zr[:], 0.0).then_inc(S.ms, 1)
+    ve.wait_ge(S.ms, 3)
+    sy.wait_ge(S.ms, 3)
+    sy.dma_start(T.D[:], T.Zb[:]).then_inc(S.d1, 16)
+    sy.wait_ge(S.d1, 16)
+    sy.dma_start(T.Id[:], T.D[0:128, :]).then_inc(S.d2, 16)
+    te.wait_ge(S.d2, 16)
+
+    bank = lambda d, c: T["P%d%d" % (d % 2, c)][:, 0:SL]
+    for d in range(NR + NB - 1):
+        blocks = [(d - c, c) for c in range(NB) if 0 <= d - c < NR]
+        for r, c in blocks:
+            if c == 0:
+                if r == s:
+                    te.wait_ge(S.rw, hu)
+                te.wait_ge(S["a%d" % r], arrived(r))
+            m = te.matmul(bank(d, c), T.Id[:], T.X[:, r, c, :], start=True, stop=(d == 0))
+            if d == 0:
+                m.then_inc(S.p0, 1)
+        for r, c in blocks:
+            if r > 0:
+                te.wait_ge(S["v%d" % c], r)
+                m = te.matmul(bank(d, c), T.Wt[:, r, 0:128], T.H[:, NB * (r - 1) + c, :], start=False, stop=(c == 0))
+            if c > 0:
+                te.wait_ge(S["v%d" % (c - 1)], r + 1)
+                m = te.matmul(bank(d, c), T.Wt[:, r, 128:256], T.H[:, NB * r + c - 1, :], start=False, stop=True)
+            if d > 0:
+                m.then_inc(S["p%d" % c], 1)
+        for r, c in blocks:
+            ve.wait_ge(S["p%d" % c], r + 1)
+            ve.tensor_tensor(T.H[:, NB * r + c, :], bank(d, c), T.Zr[:], AluOpType.max).then_inc(S["v%d" % c], 1)
+
+    for r1 in range(0, NR, 2):
+        for c in range(NB):
+            g.wait_ge(S["v%d" % c], r1 + 2)
+        g.remote_dma_fused([_tr(topo, core, [(c0[r1 + k], T.land[:, sl[s]])], off[4 * k:4 * k + 4], S.ret,
+                                T.H[:, NB * (r1 + k):NB * (r1 + k) + NB, :]) for k in range(2)], local_sem=S.ls)
+    g.wait_ge(S.ls, 16 + 8 * (NR // 2))

@@ -31,17 +31,21 @@ def _bits(mask):
 def _plan(T, topo):
     c0 = list(T.cores)
     world = range((max(topo.host(c) for c in c0) + 1) * topo.CORES_PER_HOST)
-    wa, rb = [], []
+    order = sorted(range(NR), key=lambda s: (not topo.may_write(c0[0], c0[s]), s))
+    sl = [order.index(s) for s in range(NR)]
+    wa, rb, half = [], [], []
     for r in range(NR):
         free = [c for c in world if c != c0[r] and topo.host(c) == topo.host(c0[r]) and topo.chip(c) == topo.chip(c0[r])
                 and all(topo.may_write(c, d) for d in c0)]
-        wa.append([c for c in free if topo.die(c) == topo.die(c0[r])][0])
-        rb.append([c for c in free if topo.die(c) != topo.die(c0[r])][0])
-    order = sorted(range(NR), key=lambda s: (not topo.may_write(c0[0], wa[s]), s))
-    sl = [order.index(s) for s in range(NR)]
+        near = [c for c in free if topo.die(c) == topo.die(c0[r])]
+        far = [c for c in free if topo.die(c) != topo.die(c0[r])]
+        pos = sl[r] % (NR // 2)
+        wa.append(near[0] if pos % 2 == 0 else far[0])
+        rb.append(far[0] if pos % 2 == 0 else far[1])
+        half.append(pos // 2)
     direct = [[s for s in order if s != r and topo.may_write(c0[r], wa[s])] for r in range(NR)]
     cross = [[s for s in order if not topo.may_write(c0[r], wa[s])] for r in range(NR)]
-    return c0, wa, rb, sl, direct, cross
+    return c0, wa, rb, sl, direct, cross, half
 
 
 def _tr(topo, src_core, dsts, mask_bits, sem, src):
@@ -53,7 +57,7 @@ def _tr(topo, src_core, dsts, mask_bits, sem, src):
 
 
 def rank_program(g, core, T, topo):
-    c0, wa, rb, sl, direct, cross = _plan(T, topo)
+    c0, wa, rb, sl, direct, cross, half = _plan(T, topo)
     S = T.sem
     sy, sc, ve, te = g.sync, g.scalar, g.vector, g.tensor
     wlo = lambda r: 128 if r == 0 else 0
@@ -67,6 +71,7 @@ def rank_program(g, core, T, topo):
         up = [b for b in _bits(topo.mask(core, A)) if b not in off]
         hu = len(up) // 2
         clo, dlo = sl[cross[r][0]], min(sl[s] for s in direct[r] + [r])
+        alo, blo = clo + 2 * half[r], clo + 2 * (1 - half[r])
         nlw = 16
         if r > 0:
             sy.dma_start(T.Wt[:, r, 0:128], T.wv[:]).then_inc(S.lw, 16)
@@ -83,8 +88,8 @@ def rank_program(g, core, T, topo):
         g.remote_dma_fused([_tr(topo, core, [(A, W(r))], up[:hu], S.rw, W(r)),
                             _tr(topo, core, [(Bc, W(r))], up[hu:], S.rw, W(r))], local_sem=S.ls)
         g.wait_ge(S.sxc, NB)
-        g.remote_dma_fused([_tr(topo, core, [(A, T.RX[:])], up[:hu], S.rx, T.xs[:, clo:clo + 2]),
-                            _tr(topo, core, [(Bc, T.RX[:])], up[hu:], S.rx, T.xs[:, clo + 2:clo + 4])], local_sem=S.ls)
+        g.remote_dma_fused([_tr(topo, core, [(A, T.RX[:])], up[:hu], S.rx, T.xs[:, alo:alo + 2]),
+                            _tr(topo, core, [(Bc, T.RX[:])], up[hu:], S.rx, T.xs[:, blo:blo + 2])], local_sem=S.ls)
         g.remote_dma_fused([_tr(topo, core, [(wa[d1], W(r)), (wa[d2], W(r))], off[0:4], S["a%d" % r], W(r)),
                             _tr(topo, core, [(wa[d3], W(r))], off[4:8], S["a%d" % r], W(r))], local_sem=S.ls)
         g.wait_ge(S.sxd, NB)
@@ -106,7 +111,8 @@ def rank_program(g, core, T, topo):
 
     is_a = core in wa
     s = wa.index(core) if is_a else rb.index(core)
-    mine = cross[s][0:2] if is_a else cross[s][2:4]
+    h = half[s] if is_a else 1 - half[s]
+    mine = cross[s][2 * h:2 * h + 2]
     hu = len([b for b in _bits(topo.mask(c0[s], core)) if b not in _bits(topo.mask(c0[s], wa[direct[s][0]]))]) // 2
     off = _bits(topo.mask(core, wa[mine[0]]))
     g.wait_ge(S.rw, hu)

@@ -3,6 +3,7 @@ from concourse.mybir import AluOpType
 
 NB, B, NR = 3, 512, 8
 SL = B // NR
+LATE = NR - 2
 
 SCRATCH = {
     "xin":  ("sbuf", [128, NB, NR, SL], "bfloat16"),
@@ -20,7 +21,7 @@ SCRATCH = {
     "P00":  ("psum", [128, 512], "float32"), "P01": ("psum", [128, 512], "float32"), "P02": ("psum", [128, 512], "float32"),
     "P10":  ("psum", [128, 512], "float32"), "P11": ("psum", [128, 512], "float32"), "P12": ("psum", [128, 512], "float32"),
 }
-SEMAPHORES = (["lw", "lx0", "lx1", "lx2", "sxc", "sxd", "ls", "rw", "rx", "ret", "cp0", "cp1", "cp2", "st",
+SEMAPHORES = (["lw", "lx0", "lx1", "lx2", "sxc", "sxd", "ls", "rw", "rx", "ret", "ret2", "cp0", "cp1", "cp2", "st",
                "ms", "d1", "d2", "p0", "p1", "p2", "v0", "v1", "v2"] + ["a%d" % r for r in range(NR)])
 
 
@@ -79,11 +80,17 @@ def rank_program(g, core, T, topo):
         sy.dma_start(T.Wt[:, r, 128:256], T.wh[:]).then_inc(S.lw, 16)
         for c, q in ((0, sc), (1, sy), (2, sc)):
             q.dma_start(T.xin[:, c], T.x[:, c * B:(c + 1) * B]).then_inc(S["lx%d" % c], 16)
+
+        def regroup(lo, c):
+            if r == 0 and c == 0:
+                return ve.tensor_scalar(T.xs[:, lo:lo + 4, c, :], T.xin[:, c, lo:lo + 4, :], 0.0, None, AluOpType.max)
+            return ve.tensor_copy(T.xs[:, lo:lo + 4, c, :], T.xin[:, c, lo:lo + 4, :])
+
         for c in range(NB):
             ve.wait_ge(S["lx%d" % c], 16)
-            ve.tensor_copy(T.xs[:, clo:clo + 4, c, :], T.xin[:, c, clo:clo + 4, :]).then_inc(S.sxc, 1)
+            regroup(clo, c).then_inc(S.sxc, 1)
         for c in range(NB):
-            ve.tensor_copy(T.xs[:, dlo:dlo + 4, c, :], T.xin[:, c, dlo:dlo + 4, :]).then_inc(S.sxd, 1)
+            regroup(dlo, c).then_inc(S.sxd, 1)
         g.wait_ge(S.lw, nlw)
         g.remote_dma_fused([_tr(topo, core, [(A, W(r))], up[:hu], S.rw, W(r)),
                             _tr(topo, core, [(Bc, W(r))], up[hu:], S.rw, W(r))], local_sem=S.ls)
@@ -100,8 +107,11 @@ def rank_program(g, core, T, topo):
         g.wait_ge(S.ls, 2 * len(up) + 8 + 8 + len(up))
         ve.wait_ge(S.ret, 4 * NR)
         for c, q in ((0, sy), (1, sc), (2, sy)):
-            ve.tensor_copy(T.yb[:, c], T.land[:, :, c, :]).then_inc(S["cp%d" % c], 1)
-            q.wait_ge(S["cp%d" % c], 1)
+            if r >= LATE and c == NB - 1:
+                q.wait_ge(S.ret2, 4 * NR)
+            else:
+                ve.tensor_copy(T.yb[:, c], T.land[:, :, c, :]).then_inc(S["cp%d" % c], 1)
+                q.wait_ge(S["cp%d" % c], 1)
             q.dma_start(T.y[:, c * B:(c + 1) * B], T.yb[:, c]).then_inc(S.st, 16)
         g.wait_ge(S.st, 16 * NB)
         return
@@ -144,32 +154,44 @@ def rank_program(g, core, T, topo):
     te.wait_ge(S.d2, 16)
 
     bank = lambda d, c: T["P%d%d" % (d % 2, c)][:, 0:SL]
-    for d in range(NR + NB - 1):
+    hh = lambda r, c: T.X[:, 0, 0, :] if r + c == 0 else T.H[:, NB * r + c, :]
+    if s == 0:
+        te.wait_ge(S.rw, hu)
+    te.wait_ge(S.a0, arrived(0))
+    ve.wait_ge(S.a0, arrived(0))
+    ve.tensor_copy(T.H[:, 0, :], T.X[:, 0, 0, :]).then_inc(S.v0, 1)
+    for d in range(1, NR + NB - 1):
         blocks = [(d - c, c) for c in range(NB) if 0 <= d - c < NR]
         for r, c in blocks:
             if c == 0:
                 if r == s:
                     te.wait_ge(S.rw, hu)
                 te.wait_ge(S["a%d" % r], arrived(r))
-            m = te.matmul(bank(d, c), T.Id[:], T.X[:, r, c, :], start=True, stop=(d == 0))
-            if d == 0:
-                m.then_inc(S.p0, 1)
+            te.matmul(bank(d, c), T.Id[:], T.X[:, r, c, :], start=True, stop=False)
         for r, c in blocks:
-            if r > 0:
-                te.wait_ge(S["v%d" % c], r)
-                m = te.matmul(bank(d, c), T.Wt[:, r, 0:128], T.H[:, NB * (r - 1) + c, :], start=False, stop=(c == 0))
             if c > 0:
-                te.wait_ge(S["v%d" % (c - 1)], r + 1)
-                m = te.matmul(bank(d, c), T.Wt[:, r, 128:256], T.H[:, NB * r + c - 1, :], start=False, stop=True)
-            if d > 0:
-                m.then_inc(S["p%d" % c], 1)
+                if r + c - 1 > 0:
+                    te.wait_ge(S["v%d" % (c - 1)], r + 1)
+                m = te.matmul(bank(d, c), T.Wt[:, r, 128:256], hh(r, c - 1), start=False, stop=(r == 0))
+            if r > 0:
+                if r - 1 + c > 0:
+                    te.wait_ge(S["v%d" % c], r)
+                m = te.matmul(bank(d, c), T.Wt[:, r, 0:128], hh(r - 1, c), start=False, stop=True)
+            m.then_inc(S["p%d" % c], 1)
         for r, c in blocks:
-            ve.wait_ge(S["p%d" % c], r + 1)
+            ve.wait_ge(S["p%d" % c], r + 1 if c else r)
             ve.tensor_tensor(T.H[:, NB * r + c, :], bank(d, c), T.Zr[:], AluOpType.max).then_inc(S["v%d" % c], 1)
 
-    for r1 in range(0, NR, 2):
+    for r1 in range(0, LATE, 2):
         for c in range(NB):
             g.wait_ge(S["v%d" % c], r1 + 2)
         g.remote_dma_fused([_tr(topo, core, [(c0[r1 + k], T.land[:, sl[s]])], off[4 * k:4 * k + 4], S.ret,
                                 T.H[:, NB * (r1 + k):NB * (r1 + k) + NB, :]) for k in range(2)], local_sem=S.ls)
-    g.wait_ge(S.ls, 16 + 8 * (NR // 2))
+    for c in range(NB - 1):
+        g.wait_ge(S["v%d" % c], NR)
+    g.remote_dma_fused([_tr(topo, core, [(c0[LATE + k], T.land[:, sl[s], 0:NB - 1, :])], off[4 * k:4 * k + 4], S.ret,
+                            T.H[:, NB * (LATE + k):NB * (LATE + k) + NB - 1, :]) for k in range(2)], local_sem=S.ls)
+    g.wait_ge(S["v%d" % (NB - 1)], NR)
+    g.remote_dma_fused([_tr(topo, core, [(c0[LATE + k], T.yb[:, NB - 1, sl[s], :])], off[4 * k:4 * k + 4], S.ret2,
+                            T.H[:, NB * (LATE + k) + NB - 1, :]) for k in range(2)], local_sem=S.ls)
+    g.wait_ge(S.ls, 16 + 8 * (LATE // 2) + 16)

@@ -4,6 +4,8 @@ from concourse.mybir import AluOpType
 NB, B, NR = 3, 512, 8
 SL = B // NR
 LATE = NR - 2
+WLAST = NR // 2
+IH = 64
 
 SCRATCH = {
     "xin":  ("sbuf", [128, NB, NR, SL], "bfloat16"),
@@ -14,15 +16,15 @@ SCRATCH = {
     "H":    ("sbuf", [128, NR * NB, SL], "bfloat16"),
     "land": ("sbuf", [128, NR, NB, SL], "bfloat16"),
     "yb":   ("sbuf", [128, NB, NR, SL], "bfloat16"),
-    "Zb":   ("sbuf", [128, 129], "bfloat16"),
+    "On":   ("sbuf", [128, IH], "bfloat16"),
+    "Ip":   ("sbuf", [128, IH], "bfloat16"),
     "Id":   ("sbuf", [128, 128], "bfloat16"),
     "Zr":   ("sbuf", [128, SL], "float32"),
-    "D":    ("dram", [129, 128], "bfloat16"),
     "P00":  ("psum", [128, 512], "float32"), "P01": ("psum", [128, 512], "float32"), "P02": ("psum", [128, 512], "float32"),
     "P10":  ("psum", [128, 512], "float32"), "P11": ("psum", [128, 512], "float32"), "P12": ("psum", [128, 512], "float32"),
 }
-SEMAPHORES = (["lw", "lx0", "lx1", "lx2", "sxc", "sxd", "ls", "rw", "rx", "ret", "ret2", "cp0", "cp1", "cp2", "st",
-               "ms", "d1", "d2", "p0", "p1", "p2", "v0", "v1", "v2"] + ["a%d" % r for r in range(NR)])
+SEMAPHORES = (["lw", "lx0", "lx1", "lx2", "ly0", "ly1", "ly2", "sxc", "sxd", "ls", "rw", "rx", "ret", "ret2", "cp0", "cp1", "cp2",
+               "st", "ms", "mz", "af", "idp", "p0", "p1", "p2", "v0", "v1", "v2"] + ["a%d" % r for r in range(NR)])
 
 
 def _bits(mask):
@@ -73,13 +75,20 @@ def rank_program(g, core, T, topo):
         hu = len(up) // 2
         clo, dlo = sl[cross[r][0]], min(sl[s] for s in direct[r] + [r])
         alo, blo = clo + 2 * half[r], clo + 2 * (1 - half[r])
+        ve.memset(T.On[:], 1.0).then_inc(S.ms, 1)
+        g.wait_ge(S.ms, 1)
+        g.affine_select(T.Ip[:], T.On[:], [[-1, IH]], AluOpType.is_equal, 0.0, 0, 1).then_inc(S.af, 1)
+        g.wait_ge(S.af, 1)
+        g.remote_dma_fused([_tr(topo, core, [(A, T.Id[:, 0:IH])], off + up, S.idp, T.Ip[:])], local_sem=S.ls)
         nlw = 16
         if r > 0:
             sy.dma_start(T.Wt[:, r, 0:128], T.wv[:]).then_inc(S.lw, 16)
             nlw = 32
-        sy.dma_start(T.Wt[:, r, 128:256], T.wh[:]).then_inc(S.lw, 16)
-        for c, q in ((0, sc), (1, sy), (2, sc)):
-            q.dma_start(T.xin[:, c], T.x[:, c * B:(c + 1) * B]).then_inc(S["lx%d" % c], 16)
+        sc.dma_start(T.Wt[:, r, 128:256], T.wh[:]).then_inc(S.lw, 16)
+        for lo, nm, qs in ((clo, "lx%d", (sy, sc, sy)), (dlo, "ly%d", (sc, sy, sc))):
+            for c in range(NB):
+                qs[c].dma_start(T.xin[:, c, lo:lo + 4, :],
+                                T.x[:, c * B + lo * SL:c * B + (lo + 4) * SL]).then_inc(S[nm % c], 16)
 
         def regroup(lo, c):
             if r == 0 and c == 0:
@@ -90,21 +99,41 @@ def rank_program(g, core, T, topo):
             ve.wait_ge(S["lx%d" % c], 16)
             regroup(clo, c).then_inc(S.sxc, 1)
         for c in range(NB):
+            ve.wait_ge(S["ly%d" % c], 16)
             regroup(dlo, c).then_inc(S.sxd, 1)
-        g.wait_ge(S.lw, nlw)
-        g.remote_dma_fused([_tr(topo, core, [(A, W(r))], up[:hu], S.rw, W(r)),
-                            _tr(topo, core, [(Bc, W(r))], up[hu:], S.rw, W(r))], local_sem=S.ls)
-        g.wait_ge(S.sxc, NB)
-        g.remote_dma_fused([_tr(topo, core, [(A, T.RX[:])], up[:hu], S.rx, T.xs[:, alo:alo + 2]),
-                            _tr(topo, core, [(Bc, T.RX[:])], up[hu:], S.rx, T.xs[:, blo:blo + 2])], local_sem=S.ls)
-        g.remote_dma_fused([_tr(topo, core, [(wa[d1], W(r)), (wa[d2], W(r))], off[0:4], S["a%d" % r], W(r)),
-                            _tr(topo, core, [(wa[d3], W(r))], off[4:8], S["a%d" % r], W(r))], local_sem=S.ls)
-        g.wait_ge(S.sxd, NB)
-        g.remote_dma_fused([_tr(topo, core, [(wa[d3], T.X[:, r])], off[0:4], S["a%d" % r], T.xs[:, sl[d3]]),
-                            _tr(topo, core, [(wa[d1], T.X[:, r])], off[4:6], S["a%d" % r], T.xs[:, sl[d1]]),
-                            _tr(topo, core, [(wa[d2], T.X[:, r])], off[6:8], S["a%d" % r], T.xs[:, sl[d2]]),
-                            _tr(topo, core, [(A, T.X[:, r])], up, S["a%d" % r], T.xs[:, sl[r]])], local_sem=S.ls)
-        g.wait_ge(S.ls, 2 * len(up) + 8 + 8 + len(up))
+
+        def w_relays():
+            g.wait_ge(S.lw, nlw)
+            g.remote_dma_fused([_tr(topo, core, [(A, W(r))], up[:hu], S.rw, W(r)),
+                                _tr(topo, core, [(Bc, W(r))], up[hu:], S.rw, W(r))], local_sem=S.ls)
+
+        def x_relays():
+            g.wait_ge(S.sxc, NB)
+            g.remote_dma_fused([_tr(topo, core, [(A, T.RX[:])], up[:hu], S.rx, T.xs[:, alo:alo + 2]),
+                                _tr(topo, core, [(Bc, T.RX[:])], up[hu:], S.rx, T.xs[:, blo:blo + 2])], local_sem=S.ls)
+
+        def w_direct():
+            g.remote_dma_fused([_tr(topo, core, [(wa[d1], W(r)), (wa[d2], W(r))], off[0:4], S["a%d" % r], W(r)),
+                                _tr(topo, core, [(wa[d3], W(r))], off[4:8], S["a%d" % r], W(r))], local_sem=S.ls)
+
+        def x_direct():
+            g.wait_ge(S.sxd, NB)
+            g.remote_dma_fused([_tr(topo, core, [(wa[d3], T.X[:, r])], off[0:4], S["a%d" % r], T.xs[:, sl[d3]]),
+                                _tr(topo, core, [(wa[d1], T.X[:, r])], off[4:6], S["a%d" % r], T.xs[:, sl[d1]]),
+                                _tr(topo, core, [(wa[d2], T.X[:, r])], off[6:8], S["a%d" % r], T.xs[:, sl[d2]]),
+                                _tr(topo, core, [(A, T.X[:, r])], up, S["a%d" % r], T.xs[:, sl[r]])], local_sem=S.ls)
+
+        if r < WLAST:
+            w_relays()
+            w_direct()
+            x_relays()
+            x_direct()
+        else:
+            x_relays()
+            w_relays()
+            x_direct()
+            w_direct()
+        g.wait_ge(S.ls, len(off) + len(up) + 2 * len(up) + 8 + 8 + len(up))
         ve.wait_ge(S.ret, 4 * NR)
         for c, q in ((0, sy), (1, sc), (2, sy)):
             if r >= LATE and c == NB - 1:
@@ -125,14 +154,34 @@ def rank_program(g, core, T, topo):
     mine = cross[s][2 * h:2 * h + 2]
     hu = len([b for b in _bits(topo.mask(c0[s], core)) if b not in _bits(topo.mask(c0[s], wa[direct[s][0]]))]) // 2
     off = _bits(topo.mask(core, wa[mine[0]]))
-    g.wait_ge(S.rw, hu)
-    g.remote_dma_fused([_tr(topo, core, [(wa[mine[k]], W(s))], off[4 * k:4 * k + 4], S["a%d" % s], W(s)) for k in range(2)],
-                       local_sem=S.ls)
-    g.wait_ge(S.rx, hu)
-    g.remote_dma_fused([_tr(topo, core, [(wa[mine[k]], T.X[:, s])], off[4 * k:4 * k + 4], S["a%d" % s], T.RX[:, k])
+    xr = lambda w: [r for r in range(NR) if w in cross[r]]
+    ip = (128 - IH) // len(xr(mine[0]))
+    lo = IH + ip * xr(mine[0]).index(s)
+    ve.memset(T.On[:, 0:ip], 1.0).then_inc(S.ms, 1)
+    g.wait_ge(S.ms, 1)
+    g.affine_select(T.Ip[:, 0:ip], T.On[:, 0:ip], [[-1, ip]], AluOpType.is_equal, 0.0, -lo, 1).then_inc(S.af, 1)
+    g.wait_ge(S.af, 1)
+    g.remote_dma_fused([_tr(topo, core, [(wa[mine[k]], T.Id[:, lo:lo + ip])], off[4 * k:4 * k + 4], S.idp, T.Ip[:, 0:ip])
                         for k in range(2)], local_sem=S.ls)
+
+    def fw_w():
+        g.wait_ge(S.rw, hu)
+        g.remote_dma_fused([_tr(topo, core, [(wa[mine[k]], W(s))], off[4 * k:4 * k + 4], S["a%d" % s], W(s))
+                            for k in range(2)], local_sem=S.ls)
+
+    def fw_x():
+        g.wait_ge(S.rx, hu)
+        g.remote_dma_fused([_tr(topo, core, [(wa[mine[k]], T.X[:, s])], off[4 * k:4 * k + 4], S["a%d" % s], T.RX[:, k])
+                            for k in range(2)], local_sem=S.ls)
+
+    if s < WLAST:
+        fw_w()
+        fw_x()
+    else:
+        fw_x()
+        fw_w()
     if not is_a:
-        g.wait_ge(S.ls, 16)
+        g.wait_ge(S.ls, 24)
         return
 
     def arrived(r):
@@ -142,16 +191,9 @@ def rank_program(g, core, T, topo):
             return 8
         return 4 + (4 if s == direct[r][2] else 2)
 
-    ve.memset(T.Zb[:], 0.0).then_inc(S.ms, 1)
-    ve.wait_ge(S.ms, 1)
-    ve.memset(T.Zb[:, 0:1], 1.0).then_inc(S.ms, 1)
-    ve.memset(T.Zr[:], 0.0).then_inc(S.ms, 1)
-    ve.wait_ge(S.ms, 3)
-    sy.wait_ge(S.ms, 3)
-    sy.dma_start(T.D[:], T.Zb[:]).then_inc(S.d1, 16)
-    sy.wait_ge(S.d1, 16)
-    sy.dma_start(T.Id[:], T.D[0:128, :]).then_inc(S.d2, 16)
-    te.wait_ge(S.d2, 16)
+    ve.memset(T.Zr[:], 0.0).then_inc(S.mz, 1)
+    ve.wait_ge(S.mz, 1)
+    te.wait_ge(S.idp, len(_bits(topo.mask(c0[s], core))) + 4 * len(xr(s)))
 
     bank = lambda d, c: T["P%d%d" % (d % 2, c)][:, 0:SL]
     hh = lambda r, c: T.X[:, 0, 0, :] if r + c == 0 else T.H[:, NB * r + c, :]
@@ -194,4 +236,4 @@ def rank_program(g, core, T, topo):
     g.wait_ge(S["v%d" % (NB - 1)], NR)
     g.remote_dma_fused([_tr(topo, core, [(c0[LATE + k], T.yb[:, NB - 1, sl[s], :])], off[4 * k:4 * k + 4], S.ret2,
                             T.H[:, NB * (LATE + k) + NB - 1, :]) for k in range(2)], local_sem=S.ls)
-    g.wait_ge(S.ls, 16 + 8 * (LATE // 2) + 16)
+    g.wait_ge(S.ls, 24 + 8 * (LATE // 2) + 16)

from concourse.bass import DstId, RemoteDMATransfer
from concourse.mybir import AluOpType

NB, B, NR = 3, 512, 8
SL = B // NR
LATE = NR - 2
WLAST = NR // 2
IH = 64

SCRATCH = {
    "xin":  ("sbuf", [128, NB, NR, SL], "bfloat16"),
    "xs":   ("sbuf", [128, NR, NB, SL], "bfloat16"),
    "RX":   ("sbuf", [128, 2, NB, SL], "bfloat16"),
    "X":    ("sbuf", [128, NR, NB, SL], "bfloat16"),
    "Wt":   ("sbuf", [128, NR, 256], "bfloat16"),
    "H":    ("sbuf", [128, NR * NB, SL], "bfloat16"),
    "land": ("sbuf", [128, NR, NB, SL], "bfloat16"),
    "yb":   ("sbuf", [128, NB, NR, SL], "bfloat16"),
    "On":   ("sbuf", [128, IH], "bfloat16"),
    "Ip":   ("sbuf", [128, IH], "bfloat16"),
    "Id":   ("sbuf", [128, 128], "bfloat16"),
    "Zr":   ("sbuf", [128, SL], "float32"),
    "P00":  ("psum", [128, 512], "float32"), "P01": ("psum", [128, 512], "float32"), "P02": ("psum", [128, 512], "float32"),
    "P10":  ("psum", [128, 512], "float32"), "P11": ("psum", [128, 512], "float32"), "P12": ("psum", [128, 512], "float32"),
}
SEMAPHORES = (["lw", "lx0", "lx1", "lx2", "ly0", "ly1", "ly2", "sxc", "sxd", "ls", "rw", "rx", "ret", "ret2", "cp0", "cp1", "cp2",
               "st", "ms", "mz", "af", "idp", "p0", "p1", "p2", "v0", "v1", "v2"] + ["a%d" % r for r in range(NR)])


def _bits(mask):
    return [1 << i for i in range(mask.bit_length()) if (mask >> i) & 1]


def _plan(T, topo):
    c0 = list(T.cores)
    world = range((max(topo.host(c) for c in c0) + 1) * topo.CORES_PER_HOST)
    order = sorted(range(NR), key=lambda s: (not topo.may_write(c0[0], c0[s]), s))
    sl = [order.index(s) for s in range(NR)]
    wa, rb, half = [], [], []
    for r in range(NR):
        free = [c for c in world if c != c0[r] and topo.host(c) == topo.host(c0[r]) and topo.chip(c) == topo.chip(c0[r])
                and all(topo.may_write(c, d) for d in c0)]
        near = [c for c in free if topo.die(c) == topo.die(c0[r])]
        far = [c for c in free if topo.die(c) != topo.die(c0[r])]
        pos = sl[r] % (NR // 2)
        wa.append(near[0] if pos % 2 == 0 else far[0])
        rb.append(far[0] if pos % 2 == 0 else far[1])
        half.append(pos // 2)
    direct = [[s for s in order if s != r and topo.may_write(c0[r], wa[s])] for r in range(NR)]
    cross = [[s for s in order if not topo.may_write(c0[r], wa[s])] for r in range(NR)]
    return c0, wa, rb, sl, direct, cross, half


def _tr(topo, src_core, dsts, mask_bits, sem, src):
    ids = []
    for d, _ in dsts:
        rid, pid = topo.addr(d, src_core)
        ids.append(DstId(rid=rid, pnc=pid))
    return RemoteDMATransfer(dst_ids=ids, dma_engine_mask=sum(mask_bits), remote_sem=sem, srcs=[src], dsts=[ap for _, ap in dsts])


def rank_program(g, core, T, topo):
    c0, wa, rb, sl, direct, cross, half = _plan(T, topo)
    S = T.sem
    sy, sc, ve, te = g.sync, g.scalar, g.vector, g.tensor
    wlo = lambda r: 128 if r == 0 else 0
    W = lambda r: T.Wt[:, r, wlo(r):256]

    if core in c0:
        r = c0.index(core)
        A, Bc = wa[r], rb[r]
        d1, d2, d3 = direct[r]
        off = _bits(topo.mask(core, wa[d1]))
        up = [b for b in _bits(topo.mask(core, A)) if b not in off]
        hu = len(up) // 2
        clo, dlo = sl[cross[r][0]], min(sl[s] for s in direct[r] + [r])
        alo, blo = clo + 2 * half[r], clo + 2 * (1 - half[r])
        ve.memset(T.On[:], 1.0).then_inc(S.ms, 1)
        g.wait_ge(S.ms, 1)
        g.affine_select(T.Ip[:], T.On[:], [[-1, IH]], AluOpType.is_equal, 0.0, 0, 1).then_inc(S.af, 1)
        g.wait_ge(S.af, 1)
        g.remote_dma_fused([_tr(topo, core, [(A, T.Id[:, 0:IH])], off + up, S.idp, T.Ip[:])], local_sem=S.ls)
        nlw = 16
        if r > 0:
            sy.dma_start(T.Wt[:, r, 0:128], T.wv[:]).then_inc(S.lw, 16)
            nlw = 32
        sc.dma_start(T.Wt[:, r, 128:256], T.wh[:]).then_inc(S.lw, 16)
        for lo, nm, qs in ((clo, "lx%d", (sy, sc, sy)), (dlo, "ly%d", (sc, sy, sc))):
            for c in range(NB):
                qs[c].dma_start(T.xin[:, c, lo:lo + 4, :],
                                T.x[:, c * B + lo * SL:c * B + (lo + 4) * SL]).then_inc(S[nm % c], 16)

        def regroup(lo, c):
            if r == 0 and c == 0:
                return ve.tensor_scalar(T.xs[:, lo:lo + 4, c, :], T.xin[:, c, lo:lo + 4, :], 0.0, None, AluOpType.max)
            return ve.tensor_copy(T.xs[:, lo:lo + 4, c, :], T.xin[:, c, lo:lo + 4, :])

        for c in range(NB):
            ve.wait_ge(S["lx%d" % c], 16)
            regroup(clo, c).then_inc(S.sxc, 1)
        for c in range(NB):
            ve.wait_ge(S["ly%d" % c], 16)
            regroup(dlo, c).then_inc(S.sxd, 1)

        def w_relays():
            g.wait_ge(S.lw, nlw)
            g.remote_dma_fused([_tr(topo, core, [(A, W(r))], up[:hu], S.rw, W(r)),
                                _tr(topo, core, [(Bc, W(r))], up[hu:], S.rw, W(r))], local_sem=S.ls)

        def x_relays():
            g.wait_ge(S.sxc, NB)
            g.remote_dma_fused([_tr(topo, core, [(A, T.RX[:])], up[:hu], S.rx, T.xs[:, alo:alo + 2]),
                                _tr(topo, core, [(Bc, T.RX[:])], up[hu:], S.rx, T.xs[:, blo:blo + 2])], local_sem=S.ls)

        def w_direct():
            g.remote_dma_fused([_tr(topo, core, [(wa[d1], W(r)), (wa[d2], W(r))], off[0:4], S["a%d" % r], W(r)),
                                _tr(topo, core, [(wa[d3], W(r))], off[4:8], S["a%d" % r], W(r))], local_sem=S.ls)

        def x_direct():
            g.wait_ge(S.sxd, NB)
            g.remote_dma_fused([_tr(topo, core, [(wa[d3], T.X[:, r])], off[0:4], S["a%d" % r], T.xs[:, sl[d3]]),
                                _tr(topo, core, [(wa[d1], T.X[:, r])], off[4:6], S["a%d" % r], T.xs[:, sl[d1]]),
                                _tr(topo, core, [(wa[d2], T.X[:, r])], off[6:8], S["a%d" % r], T.xs[:, sl[d2]]),
                                _tr(topo, core, [(A, T.X[:, r])], up, S["a%d" % r], T.xs[:, sl[r]])], local_sem=S.ls)

        if r < WLAST:
            w_relays()
            w_direct()
            x_relays()
            x_direct()
        else:
            x_relays()
            w_relays()
            x_direct()
            w_direct()
        g.wait_ge(S.ls, len(off) + len(up) + 2 * len(up) + 8 + 8 + len(up))
        ve.wait_ge(S.ret, 4 * NR)
        for c, q in ((0, sy), (1, sc), (2, sy)):
            if r >= LATE and c == NB - 1:
                q.wait_ge(S.ret2, 4 * NR)
            else:
                ve.tensor_copy(T.yb[:, c], T.land[:, :, c, :]).then_inc(S["cp%d" % c], 1)
                q.wait_ge(S["cp%d" % c], 1)
            q.dma_start(T.y[:, c * B:(c + 1) * B], T.yb[:, c]).then_inc(S.st, 16)
        g.wait_ge(S.st, 16 * NB)
        return

    if core not in wa and core not in rb:
        return

    is_a = core in wa
    s = wa.index(core) if is_a else rb.index(core)
    h = half[s] if is_a else 1 - half[s]
    mine = cross[s][2 * h:2 * h + 2]
    hu = len([b for b in _bits(topo.mask(c0[s], core)) if b not in _bits(topo.mask(c0[s], wa[direct[s][0]]))]) // 2
    off = _bits(topo.mask(core, wa[mine[0]]))
    xr = lambda w: [r for r in range(NR) if w in cross[r]]
    ip = (128 - IH) // len(xr(mine[0]))
    lo = IH + ip * xr(mine[0]).index(s)
    ve.memset(T.On[:, 0:ip], 1.0).then_inc(S.ms, 1)
    g.wait_ge(S.ms, 1)
    g.affine_select(T.Ip[:, 0:ip], T.On[:, 0:ip], [[-1, ip]], AluOpType.is_equal, 0.0, -lo, 1).then_inc(S.af, 1)
    g.wait_ge(S.af, 1)
    g.remote_dma_fused([_tr(topo, core, [(wa[mine[k]], T.Id[:, lo:lo + ip])], off[4 * k:4 * k + 4], S.idp, T.Ip[:, 0:ip])
                        for k in range(2)], local_sem=S.ls)

    def fw_w():
        g.wait_ge(S.rw, hu)
        g.remote_dma_fused([_tr(topo, core, [(wa[mine[k]], W(s))], off[4 * k:4 * k + 4], S["a%d" % s], W(s))
                            for k in range(2)], local_sem=S.ls)

    def fw_x():
        g.wait_ge(S.rx, hu)
        g.remote_dma_fused([_tr(topo, core, [(wa[mine[k]], T.X[:, s])], off[4 * k:4 * k + 4], S["a%d" % s], T.RX[:, k])
                            for k in range(2)], local_sem=S.ls)

    if s < WLAST:
        fw_w()
        fw_x()
    else:
        fw_x()
        fw_w()
    if not is_a:
        g.wait_ge(S.ls, 24)
        return

    def arrived(r):
        if r == s:
            return 2 * hu
        if s in cross[r]:
            return 8
        return 4 + (4 if s == direct[r][2] else 2)

    ve.memset(T.Zr[:], 0.0).then_inc(S.mz, 1)
    ve.wait_ge(S.mz, 1)
    te.wait_ge(S.idp, len(_bits(topo.mask(c0[s], core))) + 4 * len(xr(s)))

    bank = lambda d, c: T["P%d%d" % (d % 2, c)][:, 0:SL]
    hh = lambda r, c: T.X[:, 0, 0, :] if r + c == 0 else T.H[:, NB * r + c, :]
    if s == 0:
        te.wait_ge(S.rw, hu)
    te.wait_ge(S.a0, arrived(0))
    ve.wait_ge(S.a0, arrived(0))
    ve.tensor_copy(T.H[:, 0, :], T.X[:, 0, 0, :]).then_inc(S.v0, 1)
    for d in range(1, NR + NB - 1):
        blocks = [(d - c, c) for c in range(NB) if 0 <= d - c < NR]
        for r, c in blocks:
            if c == 0:
                if r == s:
                    te.wait_ge(S.rw, hu)
                te.wait_ge(S["a%d" % r], arrived(r))
            te.matmul(bank(d, c), T.Id[:], T.X[:, r, c, :], start=True, stop=False)
        for r, c in blocks:
            if c > 0:
                if r + c - 1 > 0:
                    te.wait_ge(S["v%d" % (c - 1)], r + 1)
                m = te.matmul(bank(d, c), T.Wt[:, r, 128:256], hh(r, c - 1), start=False, stop=(r == 0))
            if r > 0:
                if r - 1 + c > 0:
                    te.wait_ge(S["v%d" % c], r)
                m = te.matmul(bank(d, c), T.Wt[:, r, 0:128], hh(r - 1, c), start=False, stop=True)
            m.then_inc(S["p%d" % c], 1)
        for r, c in blocks:
            ve.wait_ge(S["p%d" % c], r + 1 if c else r)
            ve.tensor_tensor(T.H[:, NB * r + c, :], bank(d, c), T.Zr[:], AluOpType.max).then_inc(S["v%d" % c], 1)

    for r1 in range(0, LATE, 2):
        for c in range(NB):
            g.wait_ge(S["v%d" % c], r1 + 2)
        g.remote_dma_fused([_tr(topo, core, [(c0[r1 + k], T.land[:, sl[s]])], off[4 * k:4 * k + 4], S.ret,
                                T.H[:, NB * (r1 + k):NB * (r1 + k) + NB, :]) for k in range(2)], local_sem=S.ls)
    for c in range(NB - 1):
        g.wait_ge(S["v%d" % c], NR)
    g.remote_dma_fused([_tr(topo, core, [(c0[LATE + k], T.land[:, sl[s], 0:NB - 1, :])], off[4 * k:4 * k + 4], S.ret,
                            T.H[:, NB * (LATE + k):NB * (LATE + k) + NB - 1, :]) for k in range(2)], local_sem=S.ls)
    g.wait_ge(S["v%d" % (NB - 1)], NR)
    g.remote_dma_fused([_tr(topo, core, [(c0[LATE + k], T.yb[:, NB - 1, sl[s], :])], off[4 * k:4 * k + 4], S.ret2,
                            T.H[:, NB * (LATE + k) + NB - 1, :]) for k in range(2)], local_sem=S.ls)
    g.wait_ge(S.ls, 24 + 8 * (LATE // 2) + 16)
